import numpy as np
import ml_dtypes


def mxq(x, axis, fmt="e4m3"):
    dtype, down = {"e4m3": (ml_dtypes.float8_e4m3fn, 7), "e5m2": (ml_dtypes.float8_e5m2, 14)}[fmt]
    v = np.moveaxis(np.asarray(x, np.float32).astype(ml_dtypes.bfloat16).astype(np.float64), axis, -1)
    blocks = v.reshape(v.shape[:-1] + (-1, 32))
    amax = np.abs(blocks).max(-1, keepdims=True)
    byte = np.maximum(np.where(amax > 0, np.frexp(amax)[1] - 1 + 127, 0) - down, 1)
    scale = np.exp2(byte - 127.0)
    codes = (blocks / scale).astype(np.float32).astype(dtype).astype(np.float64)
    return np.moveaxis((codes * scale).reshape(v.shape), -1, axis)


WIDE = False


def mx_kscale(k):
    if not WIDE:
        return np.ones(k)
    levels = np.array([30, -30])
    if k % 512:
        return np.exp2(np.random.permutation(np.resize(levels, k // 32))).repeat(32)
    a = np.empty((k // 512, 16))
    for p in range(k // 512):
        a[p, :8] = np.random.permutation(np.resize(levels, 8))
        for g in range(8):
            far = levels[np.abs(levels - a[p, g]) >= 10]
            a[p, g + 8] = far[np.random.randint(len(far))]
    return np.exp2(a.ravel()).repeat(32)


def f64(x):
    return np.asarray(x).astype(np.float64)


def striped(idx):
    return np.tile(np.asarray(idx).reshape(-1, 16).T, (8, 1)).astype(np.uint16)


def unstriped(offs):
    return offs[:16].T.reshape(-1).astype(np.int64)


E2M1 = np.array([0.0, 0.5, 1.0, 1.5, 2.0, 3.0, 4.0, 6.0, -0.0, -0.5, -1.0, -1.5, -2.0, -3.0, -4.0, -6.0])


def pack_weight(w, fmt):
    k, n = w.shape
    w = f64(np.asarray(w, np.float32).astype(ml_dtypes.bfloat16)).reshape(k // 32, 32, n)
    amax = np.abs(w).max(1)
    if fmt == "e4m3":
        byte = np.frexp(amax)[1] - 1 + 127 - 7
    else:
        mant, ex = np.frexp(amax / 6.0)
        byte = np.where(mant > 0.5, ex, ex - 1) + 127
    byte = np.clip(np.where(amax > 0, byte, 1), 1, 254)
    scaled = (w * np.exp2(127.0 - byte)[:, None, :]).reshape(k, n).astype(np.float32)
    by_word = np.ascontiguousarray(scaled.reshape(k // 512, 128, 4, n).transpose(0, 1, 3, 2))
    if fmt == "e4m3":
        words = by_word.astype(ml_dtypes.float8_e4m3fn).view(np.uint8)
    else:
        c = by_word.astype(ml_dtypes.float4_e2m1fn).view(np.uint8) & 0xF
        words = (c[..., 0::2] | (c[..., 1::2] << 4)).reshape(k // 512, 128, 2 * n)
    return np.ascontiguousarray(words), np.ascontiguousarray(byte.astype(np.uint8).reshape(k // 512, 16, n))


def unpack_weight(words, scales, fmt):
    g, _, n = scales.shape
    words = np.ascontiguousarray(words).reshape(g, 128, n, -1)
    if fmt == "e4m3":
        vals = words.view(ml_dtypes.float8_e4m3fn).astype(np.float64)
    else:
        nib = np.empty((g, 128, n, 4), np.uint8)
        nib[..., 0::2] = words & 0xF
        nib[..., 1::2] = words >> 4
        vals = E2M1[nib]
    vals = vals * np.repeat(np.exp2(scales.astype(np.float64) - 127.0), 8, axis=1)[..., None]
    return vals.transpose(0, 1, 3, 2).reshape(g * 512, n)


def bf(x):
    return np.asarray(x, np.float32).astype(ml_dtypes.bfloat16)


def planes(Y):
    r, m = Y.shape
    b = f64(bf(Y)).reshape(r // 32, 32, m)
    amax = np.abs(b).max(1)
    byte = np.clip(np.where(amax > 0, np.frexp(amax)[1] - 1 + 127 - 7, 1), 1, 254)
    codes = (b * np.exp2(127.0 - byte)[:, None, :]).reshape(r, m).astype(np.float32).astype(ml_dtypes.float8_e4m3fn).view(np.uint8)
    words = codes.reshape(r // 512, 128, 4, m).transpose(0, 1, 3, 2)
    return np.ascontiguousarray(words), np.ascontiguousarray(byte.astype(np.uint8).reshape(r // 512, 16, m))


N, K, T, J = 512, 512, 2048, 512


def setup_inputs():
    n = np.random.standard_normal
    idx = np.random.permutation(T)[:J]
    fn = mx_kscale(N)
    wp = pack_weight(n((N, K)) * 1 / np.sqrt(N) * fn[:, None], "e4m3")
    return {
        "g": (n((N, T))).astype(np.float32),
        "sv": (n((N, T))).astype(np.float32),
        "inv": (np.random.uniform(0.5, 2.0, (N, 1)) / fn[:, None]).astype(np.float32),
        "w_words": wp[0],
        "w_scales": wp[1],
        "res": (0.5 * n((K, J))).astype(np.float32),
        "offs": striped(idx),
    }


def reference(g, sv, inv, w_words, w_scales, res, offs):
    idx = unstriped(offs)
    wu = unpack_weight(w_words, w_scales, "e4m3")
    d = (f64(g)[:, idx] - f64(sv)[:, idx] * np.mean(f64(g)[:, idx] * f64(sv)[:, idx], axis=1, keepdims=True)) * f64(inv)
    dq = mxq(d, 0, "e5m2")
    p = wu.T @ dq
    y = p + f64(res)
    words, scales = planes(y)
    return y, words, scales

@@ -1,0 +1,149 @@
+from contextlib import ExitStack
+
+import concourse.mybir as mybir
+
+N, K, T, J = 512, 512, 2048, 512
+FLOPS = 2 * N * K * J
+
+F32 = mybir.dt.float32
+BF16 = mybir.dt.bfloat16
+I32 = mybir.dt.int32
+U16 = mybir.dt.uint16
+U8 = mybir.dt.uint8
+E4M3X4 = mybir.dt.float8_e4m3fn_x4
+E5M2X4 = mybir.dt.float8_e5m2_x4
+MULT = mybir.AluOpType.mult
+ADD = mybir.AluOpType.add
+COPY = mybir.ActivationFunctionType.Copy
+
+P = 128
+PACK = 4
+HALF = J // 2
+HALVES = (slice(0, HALF), slice(HALF, J))
+
+
+def tile_list_evened_features_back_pl_kernel(tc, g, sv, inv, w_words, w_scales, res, offs, out_0, out_1, out_2):
+    nc = tc.nc
+    with ExitStack() as ctx:
+        keep = ctx.enter_context(tc.tile_pool(name="keep", bufs=1))
+        psum = ctx.enter_context(tc.psum_pool(name="psum", bufs=1))
+
+        offsets = keep.tile([P, J // 16], U16, name="offsets")
+        g_rows = [keep.tile([P, T], F32, name=f"g_rows{t}") for t in range(PACK)]
+        sv_rows = [keep.tile([P, T], F32, name=f"sv_rows{t}") for t in range(PACK)]
+        inv_sb = keep.tile([P, PACK], F32, name="inv_sb")
+        w_raw = keep.tile([P, K], I32, name="w_raw", align_bytes=64)
+        w_scale_raw = keep.tile([P, K], U8, name="w_scale_raw", align_bytes=64)
+        res_sb = keep.tile([P, PACK, J], F32, name="res_sb")
+
+        g_dealt = g.rearrange("(p t) c -> p t c", t=PACK)
+        sv_dealt = sv.rearrange("(p t) c -> p t c", t=PACK)
+
+        nc.vector.memset(w_scale_raw[:].bitcast(I32), 0)
+        nc.sync.dma_start(out=sv_rows[0][:], in_=sv_dealt[:, 0, :])
+        nc.sync.dma_start(offsets[:], offs)
+        nc.scalar.dma_start(out=inv_sb[:], in_=inv.rearrange("(p t) o -> p (t o)", t=PACK))
+        for q in range(4):
+            nc.scalar.dma_start(
+                out=w_scale_raw[32 * q : 32 * q + 4, :].bitcast(I32),
+                in_=w_scales[0, 4 * q : 4 * q + 4, :].bitcast(I32),
+            )
+        nc.sync.dma_start(out=g_rows[0][:], in_=g_dealt[:, 0, :])
+        for t in range(1, PACK):
+            nc.sync.dma_start(out=sv_rows[t][:], in_=sv_dealt[:, t, :])
+            nc.sync.dma_start(out=g_rows[t][:], in_=g_dealt[:, t, :])
+        nc.sync.dma_start(out=w_raw[:], in_=w_words[0].rearrange("p c r -> p (c r)").bitcast(I32))
+        nc.sync.dma_start(out=res_sb[:], in_=res.rearrange("(p t) j -> p t j", t=PACK))
+
+        d_grouped = [keep.tile([P, HALF, PACK], BF16, name=f"d_grouped{h}", align_bytes=64) for h in range(2)]
+        d_codes = keep.tile([P, J], I32, name="d_codes", align_bytes=64)
+        d_scale = keep.tile([P, J], U8, name="d_scale", align_bytes=64)
+        for t in range(PACK):
+            sv_picked = keep.tile([P, J], F32, name=f"sv_picked{t}")
+            g_picked = keep.tile([P, J], F32, name=f"g_picked{t}")
+            product = keep.tile([P, J], F32, name=f"product{t}", tag=f"product{t}", align_bytes=64)
+            neg_mean = keep.tile([P, 1], F32, name=f"neg_mean{t}")
+            nc.vector.tensor_copy(sv_picked[:], sv_rows[t][:].indirect(offsets[:]))
+            nc.vector.tensor_copy(g_picked[:], g_rows[t][:].indirect(offsets[:]))
+            nc.vector.scalar_tensor_tensor(
+                out=product[:], in0=g_picked[:], scalar=-1.0 / J, in1=sv_picked[:],
+                op0=MULT, op1=MULT, accum_out=neg_mean[:],
+            )
+            if t == 1:
+                w_scale = keep.tile([P, K], U8, name="w_scale", tag="product1", align_bytes=64)
+                nc.vector.tensor_copy(
+                    out=w_scale[:].rearrange("p (t m) -> p t m", t=PACK),
+                    in_=w_scale_raw[:].rearrange("p (m t) -> p t m", t=PACK),
+                )
+            if t == PACK - 1:
+                w_codes = keep.tile([P, K], I32, name="w_codes", tag="product3", align_bytes=64)
+                nc.vector.tensor_copy(
+                    out=w_codes[:].rearrange("p (t m) -> p t m", t=PACK),
+                    in_=w_raw[:].rearrange("p (m t) -> p t m", t=PACK),
+                )
+            factor = inv_sb[:, t : t + 1]
+            evened = [keep.tile([P, HALF], F32, name=f"evened{t}_{h}") for h in range(2)]
+            for h in range(2):
+                nc.vector.scalar_tensor_tensor(
+                    out=evened[h][:], in0=sv_picked[:, HALVES[h]], scalar=neg_mean[:], in1=g_picked[:, HALVES[h]],
+                    op0=MULT, op1=ADD,
+                )
+            nc.scalar.activation(out=d_grouped[0][:, :, t], in_=evened[0][:], func=COPY, scale=factor)
+            if t < 2:
+                nc.scalar.activation(out=d_grouped[1][:, :, t], in_=evened[1][:], func=COPY, scale=factor)
+            else:
+                nc.vector.tensor_scalar(
+                    out=d_grouped[1][:, :, t], in0=evened[1][:], scalar1=factor, scalar2=None, op0=MULT
+                )
+        for h in (1, 0):
+            nc.vector.quantize_mx(
+                out=d_codes[:, HALVES[h]].bitcast(E5M2X4),
+                scales=d_scale[:, HALVES[h]],
+                in_=d_grouped[h][:].rearrange("p j t -> p (j t)"),
+            )
+
+        y_pairs = [keep.tile([P, 2, J], F32, name=f"y_pair{u}") for u in range(2)]
+        y_grouped = [keep.tile([P, HALF, PACK], BF16, name=f"y_grouped{h}", align_bytes=64) for h in range(2)]
+        y_codes = keep.tile([P, J], I32, name="y_codes", align_bytes=64)
+        y_scale = keep.tile([P, J], U8, name="y_scale", align_bytes=64)
+        out_dealt = out_0.rearrange("(p t) j -> p t j", t=PACK)
+        for t in range(PACK):
+            acc = psum.tile([P, J], F32, name=f"acc{t}")
+            cols = slice(P * t, P * (t + 1))
+            nc.tensor.matmul_mx(
+                out=acc[:],
+                lhsT=w_codes[:, cols].bitcast(E4M3X4),
+                lhsT_scale=w_scale[:, cols],
+                rhs=d_codes[:].bitcast(E5M2X4),
+                rhs_scale=d_scale[:],
+                start=True,
+                stop=True,
+            )
+            u, e = divmod(t, 2)
+            nc.vector.tensor_tensor(out=y_pairs[u][:, e, :], in0=acc[:], in1=res_sb[:, t, :], op=ADD)
+            if t == 1:
+                nc.sync.dma_start(out=out_dealt[:, 0:2, :], in_=y_pairs[0][:])
+                for h in range(2):
+                    nc.scalar.copy(
+                        out=y_grouped[h][:, :, 0:2], in_=y_pairs[0][:, :, HALVES[h]].rearrange("p e j -> p j e")
+                    )
+            if t >= 2:
+                nc.sync.dma_start(out=out_dealt[:, t, :], in_=y_pairs[1][:, e, :])
+        for h in range(2):
+            nc.vector.tensor_copy(
+                out=y_grouped[h][:, :, 2:4], in_=y_pairs[1][:, :, HALVES[h]].rearrange("p e j -> p j e")
+            )
+        words = out_1[0].rearrange("p c r -> p (c r)").bitcast(I32)
+        for h in range(2):
+            nc.vector.quantize_mx(
+                out=y_codes[:, HALVES[h]].bitcast(E4M3X4),
+                scales=y_scale[:, HALVES[h]],
+                in_=y_grouped[h][:].rearrange("p j t -> p (j t)"),
+            )
+            nc.sync.dma_start(out=words[:, HALVES[h]], in_=y_codes[:, HALVES[h]])
+        for q in range(4):
+            queue = nc.scalar if q % 2 == 0 else nc.sync
+            queue.dma_start(
+                out=out_2[0, 4 * q : 4 * q + 4, :].bitcast(I32),
+                in_=y_scale[32 * q : 32 * q + 4, :].bitcast(I32),
+            )

@@ -43,24 +43,26 @@ def tile_list_evened_features_back_pl_kernel(tc, g, sv, inv, w_words, w_scales, 
         nc.sync.dma_start(out=sv_rows[0][:], in_=sv_dealt[:, 0, :])
         nc.sync.dma_start(offsets[:], offs)
         nc.scalar.dma_start(out=inv_sb[:], in_=inv.rearrange("(p t) o -> p (t o)", t=PACK))
-        for q in range(4):
-            nc.scalar.dma_start(
-                out=w_scale_raw[32 * q : 32 * q + 4, :].bitcast(I32),
-                in_=w_scales[0, 4 * q : 4 * q + 4, :].bitcast(I32),
-            )
         nc.sync.dma_start(out=g_rows[0][:], in_=g_dealt[:, 0, :])
         for t in range(1, PACK):
             nc.sync.dma_start(out=sv_rows[t][:], in_=sv_dealt[:, t, :])
             nc.sync.dma_start(out=g_rows[t][:], in_=g_dealt[:, t, :])
+        for q in range(4):
+            nc.sync.dma_start(
+                out=w_scale_raw[32 * q : 32 * q + 4, :].bitcast(I32),
+                in_=w_scales[0, 4 * q : 4 * q + 4, :].bitcast(I32),
+            )
         nc.sync.dma_start(out=w_raw[:], in_=w_words[0].rearrange("p c r -> p (c r)").bitcast(I32))
         nc.sync.dma_start(out=res_sb[:], in_=res.rearrange("(p t) j -> p t j", t=PACK))
 
-        d_grouped = [keep.tile([P, HALF, PACK], BF16, name=f"d_grouped{h}", align_bytes=64) for h in range(2)]
+        d_grouped = [keep.tile([P, HALF, PACK], BF16, name=f"d_grouped{h}", tag=f"d_grouped{h}", align_bytes=64) for h in range(2)]
         d_codes = keep.tile([P, J], I32, name="d_codes", align_bytes=64)
         d_scale = keep.tile([P, J], U8, name="d_scale", align_bytes=64)
+        scale_by_slice = w_scale_raw[:].rearrange("p (m t) -> p t m", t=PACK)
+        w_by_slice = w_raw[:].rearrange("p (m t) -> p t m", t=PACK)
         for t in range(PACK):
             sv_picked = keep.tile([P, J], F32, name=f"sv_picked{t}")
-            g_picked = keep.tile([P, J], F32, name=f"g_picked{t}")
+            g_picked = keep.tile([P, J], F32, name=f"g_picked{t}", tag=f"g_picked{t}", align_bytes=64)
             product = keep.tile([P, J], F32, name=f"product{t}", tag=f"product{t}", align_bytes=64)
             neg_mean = keep.tile([P, 1], F32, name=f"neg_mean{t}")
             nc.vector.tensor_copy(sv_picked[:], sv_rows[t][:].indirect(offsets[:]))
@@ -69,38 +71,44 @@ def tile_list_evened_features_back_pl_kernel(tc, g, sv, inv, w_words, w_scales, 
                 out=product[:], in0=g_picked[:], scalar=-1.0 / J, in1=sv_picked[:],
                 op0=MULT, op1=MULT, accum_out=neg_mean[:],
             )
-            if t == 1:
-                w_scale = keep.tile([P, K], U8, name="w_scale", tag="product1", align_bytes=64)
-                nc.vector.tensor_copy(
-                    out=w_scale[:].rearrange("p (t m) -> p t m", t=PACK),
-                    in_=w_scale_raw[:].rearrange("p (m t) -> p t m", t=PACK),
-                )
-            if t == PACK - 1:
-                w_codes = keep.tile([P, K], I32, name="w_codes", tag="product3", align_bytes=64)
-                nc.vector.tensor_copy(
-                    out=w_codes[:].rearrange("p (t m) -> p t m", t=PACK),
-                    in_=w_raw[:].rearrange("p (m t) -> p t m", t=PACK),
-                )
             factor = inv_sb[:, t : t + 1]
-            evened = [keep.tile([P, HALF], F32, name=f"evened{t}_{h}") for h in range(2)]
-            for h in range(2):
+            if t < PACK - 1:
+                evened = keep.tile([P, J], F32, name=f"evened{t}", tag="evened")
                 nc.vector.scalar_tensor_tensor(
-                    out=evened[h][:], in0=sv_picked[:, HALVES[h]], scalar=neg_mean[:], in1=g_picked[:, HALVES[h]],
-                    op0=MULT, op1=ADD,
+                    out=evened[:], in0=sv_picked[:], scalar=neg_mean[:], in1=g_picked[:], op0=MULT, op1=ADD
                 )
-            nc.scalar.activation(out=d_grouped[0][:, :, t], in_=evened[0][:], func=COPY, scale=factor)
-            if t < 2:
-                nc.scalar.activation(out=d_grouped[1][:, :, t], in_=evened[1][:], func=COPY, scale=factor)
+                for h in range(2):
+                    nc.scalar.activation(out=d_grouped[h][:, :, t], in_=evened[:, HALVES[h]], func=COPY, scale=factor)
             else:
-                nc.vector.tensor_scalar(
-                    out=d_grouped[1][:, :, t], in0=evened[1][:], scalar1=factor, scalar2=None, op0=MULT
+                scale_early = keep.tile([P, 2, P], U8, name="scale_early", tag="product3", align_bytes=64)
+                nc.vector.tensor_copy(out=scale_early[:], in_=scale_by_slice[:, 0:2, :])
+                halves = [
+                    keep.tile([P, HALF], F32, name="evened_low"),
+                    keep.tile([P, HALF], F32, name="evened_high", tag="evened"),
+                ]
+                for h in range(2):
+                    nc.vector.scalar_tensor_tensor(
+                        out=halves[h][:], in0=sv_picked[:, HALVES[h]], scalar=neg_mean[:], in1=g_picked[:, HALVES[h]],
+                        op0=MULT, op1=ADD,
+                    )
+                w_codes = keep.tile([P, PACK, P], I32, name="w_codes", tag="g_picked3", align_bytes=64)
+                nc.vector.tensor_copy(
+                    out=w_codes[:].rearrange("p t (c i) -> p c t i", i=4),
+                    in_=w_by_slice.rearrange("p t (c i) -> p c t i", i=4),
                 )
-        for h in (1, 0):
+                nc.scalar.activation(out=d_grouped[0][:, :, t], in_=halves[0][:], func=COPY, scale=factor)
+                nc.vector.tensor_scalar(
+                    out=d_grouped[1][:, :, t], in0=halves[1][:], scalar1=factor, scalar2=None, op0=MULT
+                )
+        for h in range(2):
             nc.vector.quantize_mx(
                 out=d_codes[:, HALVES[h]].bitcast(E5M2X4),
                 scales=d_scale[:, HALVES[h]],
                 in_=d_grouped[h][:].rearrange("p j t -> p (j t)"),
             )
+        scale_late = keep.tile([P, 2, P], U8, name="scale_late", tag="d_grouped1", align_bytes=64)
+        nc.vector.tensor_copy(out=scale_late[:], in_=scale_by_slice[:, 2:4, :])
+        scale_slices = [half[:, e, :] for half in (scale_early, scale_late) for e in range(2)]
 
         y_pairs = [keep.tile([P, 2, J], F32, name=f"y_pair{u}") for u in range(2)]
         y_grouped = [keep.tile([P, HALF, PACK], BF16, name=f"y_grouped{h}", align_bytes=64) for h in range(2)]
@@ -109,26 +117,24 @@ def tile_list_evened_features_back_pl_kernel(tc, g, sv, inv, w_words, w_scales, 
         out_dealt = out_0.rearrange("(p t) j -> p t j", t=PACK)
         for t in range(PACK):
             acc = psum.tile([P, J], F32, name=f"acc{t}")
-            cols = slice(P * t, P * (t + 1))
             nc.tensor.matmul_mx(
                 out=acc[:],
-                lhsT=w_codes[:, cols].bitcast(E4M3X4),
-                lhsT_scale=w_scale[:, cols],
+                lhsT=w_codes[:, t, :].bitcast(E4M3X4),
+                lhsT_scale=scale_slices[t],
                 rhs=d_codes[:].bitcast(E5M2X4),
                 rhs_scale=d_scale[:],
                 start=True,
                 stop=True,
             )
             u, e = divmod(t, 2)
-            nc.vector.tensor_tensor(out=y_pairs[u][:, e, :], in0=acc[:], in1=res_sb[:, t, :], op=ADD)
+            for part in HALVES if t == PACK - 1 else (slice(0, J),):
+                nc.vector.tensor_tensor(out=y_pairs[u][:, e, part], in0=acc[:, part], in1=res_sb[:, t, part], op=ADD)
+            nc.sync.dma_start(out=out_dealt[:, t, :], in_=y_pairs[u][:, e, :])
             if t == 1:
-                nc.sync.dma_start(out=out_dealt[:, 0:2, :], in_=y_pairs[0][:])
                 for h in range(2):
                     nc.scalar.copy(
                         out=y_grouped[h][:, :, 0:2], in_=y_pairs[0][:, :, HALVES[h]].rearrange("p e j -> p j e")
                     )
-            if t >= 2:
-                nc.sync.dma_start(out=out_dealt[:, t, :], in_=y_pairs[1][:, e, :])
         for h in range(2):
             nc.vector.tensor_copy(
                 out=y_grouped[h][:, :, 2:4], in_=y_pairs[1][:, :, HALVES[h]].rearrange("p e j -> p j e")

from contextlib import ExitStack

import concourse.mybir as mybir

N, K, T, J = 512, 512, 2048, 512
FLOPS = 2 * N * K * J

F32 = mybir.dt.float32
BF16 = mybir.dt.bfloat16
I32 = mybir.dt.int32
U16 = mybir.dt.uint16
U8 = mybir.dt.uint8
E4M3X4 = mybir.dt.float8_e4m3fn_x4
E5M2X4 = mybir.dt.float8_e5m2_x4
MULT = mybir.AluOpType.mult
ADD = mybir.AluOpType.add
COPY = mybir.ActivationFunctionType.Copy

P = 128
PACK = 4
HALF = J // 2
HALVES = (slice(0, HALF), slice(HALF, J))


def tile_list_evened_features_back_pl_kernel(tc, g, sv, inv, w_words, w_scales, res, offs, out_0, out_1, out_2):
    nc = tc.nc
    with ExitStack() as ctx:
        keep = ctx.enter_context(tc.tile_pool(name="keep", bufs=1))
        psum = ctx.enter_context(tc.psum_pool(name="psum", bufs=1))

        offsets = keep.tile([P, J // 16], U16, name="offsets")
        g_rows = [keep.tile([P, T], F32, name=f"g_rows{t}") for t in range(PACK)]
        sv_rows = [keep.tile([P, T], F32, name=f"sv_rows{t}") for t in range(PACK)]
        inv_sb = keep.tile([P, PACK], F32, name="inv_sb")
        w_raw = keep.tile([P, K], I32, name="w_raw", align_bytes=64)
        w_scale_raw = keep.tile([P, K], U8, name="w_scale_raw", align_bytes=64)
        res_sb = keep.tile([P, PACK, J], F32, name="res_sb")

        g_dealt = g.rearrange("(p t) c -> p t c", t=PACK)
        sv_dealt = sv.rearrange("(p t) c -> p t c", t=PACK)

        nc.vector.memset(w_scale_raw[:].bitcast(I32), 0)
        nc.sync.dma_start(out=sv_rows[0][:], in_=sv_dealt[:, 0, :])
        nc.sync.dma_start(offsets[:], offs)
        nc.scalar.dma_start(out=inv_sb[:], in_=inv.rearrange("(p t) o -> p (t o)", t=PACK))
        nc.sync.dma_start(out=g_rows[0][:], in_=g_dealt[:, 0, :])
        for t in range(1, PACK):
            nc.sync.dma_start(out=sv_rows[t][:], in_=sv_dealt[:, t, :])
            nc.sync.dma_start(out=g_rows[t][:], in_=g_dealt[:, t, :])
        for q in range(4):
            nc.sync.dma_start(
                out=w_scale_raw[32 * q : 32 * q + 4, :].bitcast(I32),
                in_=w_scales[0, 4 * q : 4 * q + 4, :].bitcast(I32),
            )
        nc.sync.dma_start(out=w_raw[:], in_=w_words[0].rearrange("p c r -> p (c r)").bitcast(I32))
        nc.sync.dma_start(out=res_sb[:], in_=res.rearrange("(p t) j -> p t j", t=PACK))

        d_grouped = [keep.tile([P, HALF, PACK], BF16, name=f"d_grouped{h}", tag=f"d_grouped{h}", align_bytes=64) for h in range(2)]
        d_codes = keep.tile([P, J], I32, name="d_codes", align_bytes=64)
        d_scale = keep.tile([P, J], U8, name="d_scale", align_bytes=64)
        scale_by_slice = w_scale_raw[:].rearrange("p (m t) -> p t m", t=PACK)
        w_by_slice = w_raw[:].rearrange("p (m t) -> p t m", t=PACK)
        for t in range(PACK):
            sv_picked = keep.tile([P, J], F32, name=f"sv_picked{t}")
            g_picked = keep.tile([P, J], F32, name=f"g_picked{t}", tag=f"g_picked{t}", align_bytes=64)
            product = keep.tile([P, J], F32, name=f"product{t}", tag=f"product{t}", align_bytes=64)
            neg_mean = keep.tile([P, 1], F32, name=f"neg_mean{t}")
            nc.vector.tensor_copy(sv_picked[:], sv_rows[t][:].indirect(offsets[:]))
            nc.vector.tensor_copy(g_picked[:], g_rows[t][:].indirect(offsets[:]))
            nc.vector.scalar_tensor_tensor(
                out=product[:], in0=g_picked[:], scalar=-1.0 / J, in1=sv_picked[:],
                op0=MULT, op1=MULT, accum_out=neg_mean[:],
            )
            factor = inv_sb[:, t : t + 1]
            if t < PACK - 1:
                evened = keep.tile([P, J], F32, name=f"evened{t}", tag="evened")
                nc.vector.scalar_tensor_tensor(
                    out=evened[:], in0=sv_picked[:], scalar=neg_mean[:], in1=g_picked[:], op0=MULT, op1=ADD
                )
                for h in range(2):
                    nc.scalar.activation(out=d_grouped[h][:, :, t], in_=evened[:, HALVES[h]], func=COPY, scale=factor)
            else:
                scale_early = keep.tile([P, 2, P], U8, name="scale_early", tag="product3", align_bytes=64)
                nc.vector.tensor_copy(out=scale_early[:], in_=scale_by_slice[:, 0:2, :])
                halves = [
                    keep.tile([P, HALF], F32, name="evened_low"),
                    keep.tile([P, HALF], F32, name="evened_high", tag="evened"),
                ]
                for h in range(2):
                    nc.vector.scalar_tensor_tensor(
                        out=halves[h][:], in0=sv_picked[:, HALVES[h]], scalar=neg_mean[:], in1=g_picked[:, HALVES[h]],
                        op0=MULT, op1=ADD,
                    )
                w_codes = keep.tile([P, PACK, P], I32, name="w_codes", tag="g_picked3", align_bytes=64)
                nc.vector.tensor_copy(
                    out=w_codes[:].rearrange("p t (c i) -> p c t i", i=4),
                    in_=w_by_slice.rearrange("p t (c i) -> p c t i", i=4),
                )
                nc.scalar.activation(out=d_grouped[0][:, :, t], in_=halves[0][:], func=COPY, scale=factor)
                nc.vector.tensor_scalar(
                    out=d_grouped[1][:, :, t], in0=halves[1][:], scalar1=factor, scalar2=None, op0=MULT
                )
        for h in range(2):
            nc.vector.quantize_mx(
                out=d_codes[:, HALVES[h]].bitcast(E5M2X4),
                scales=d_scale[:, HALVES[h]],
                in_=d_grouped[h][:].rearrange("p j t -> p (j t)"),
            )
        scale_late = keep.tile([P, 2, P], U8, name="scale_late", tag="d_grouped1", align_bytes=64)
        nc.vector.tensor_copy(out=scale_late[:], in_=scale_by_slice[:, 2:4, :])
        scale_slices = [half[:, e, :] for half in (scale_early, scale_late) for e in range(2)]

        y_pairs = [keep.tile([P, 2, J], F32, name=f"y_pair{u}") for u in range(2)]
        y_grouped = [keep.tile([P, HALF, PACK], BF16, name=f"y_grouped{h}", align_bytes=64) for h in range(2)]
        y_codes = keep.tile([P, J], I32, name="y_codes", align_bytes=64)
        y_scale = keep.tile([P, J], U8, name="y_scale", align_bytes=64)
        out_dealt = out_0.rearrange("(p t) j -> p t j", t=PACK)
        for t in range(PACK):
            acc = psum.tile([P, J], F32, name=f"acc{t}")
            nc.tensor.matmul_mx(
                out=acc[:],
                lhsT=w_codes[:, t, :].bitcast(E4M3X4),
                lhsT_scale=scale_slices[t],
                rhs=d_codes[:].bitcast(E5M2X4),
                rhs_scale=d_scale[:],
                start=True,
                stop=True,
            )
            u, e = divmod(t, 2)
            for part in HALVES if t == PACK - 1 else (slice(0, J),):
                nc.vector.tensor_tensor(out=y_pairs[u][:, e, part], in0=acc[:, part], in1=res_sb[:, t, part], op=ADD)
            nc.sync.dma_start(out=out_dealt[:, t, :], in_=y_pairs[u][:, e, :])
            if t == 1:
                for h in range(2):
                    nc.scalar.copy(
                        out=y_grouped[h][:, :, 0:2], in_=y_pairs[0][:, :, HALVES[h]].rearrange("p e j -> p j e")
                    )
        for h in range(2):
            nc.vector.tensor_copy(
                out=y_grouped[h][:, :, 2:4], in_=y_pairs[1][:, :, HALVES[h]].rearrange("p e j -> p j e")
            )
        words = out_1[0].rearrange("p c r -> p (c r)").bitcast(I32)
        for h in range(2):
            nc.vector.quantize_mx(
                out=y_codes[:, HALVES[h]].bitcast(E4M3X4),
                scales=y_scale[:, HALVES[h]],
                in_=y_grouped[h][:].rearrange("p j t -> p (j t)"),
            )
            nc.sync.dma_start(out=words[:, HALVES[h]], in_=y_codes[:, HALVES[h]])
        for q in range(4):
            queue = nc.scalar if q % 2 == 0 else nc.sync
            queue.dma_start(
                out=out_2[0, 4 * q : 4 * q + 4, :].bitcast(I32),
                in_=y_scale[32 * q : 32 * q + 4, :].bitcast(I32),
            )
